import numpy as np
import ml_dtypes


def mxq(x, axis, fmt="e4m3"):
    dtype, down = {"e4m3": (ml_dtypes.float8_e4m3fn, 7), "e5m2": (ml_dtypes.float8_e5m2, 14)}[fmt]
    v = np.moveaxis(np.asarray(x, np.float32).astype(ml_dtypes.bfloat16).astype(np.float64), axis, -1)
    blocks = v.reshape(v.shape[:-1] + (-1, 32))
    amax = np.abs(blocks).max(-1, keepdims=True)
    byte = np.maximum(np.where(amax > 0, np.frexp(amax)[1] - 1 + 127, 0) - down, 1)
    scale = np.exp2(byte - 127.0)
    codes = (blocks / scale).astype(np.float32).astype(dtype).astype(np.float64)
    return np.moveaxis((codes * scale).reshape(v.shape), -1, axis)


WIDE = False


def mx_kscale(k):
    if not WIDE:
        return np.ones(k)
    levels = np.array([10, -10, 5, -5, 0])
    if k % 512:
        return np.exp2(np.random.permutation(np.resize(levels, k // 32))).repeat(32)
    a = np.empty((k // 512, 16))
    for p in range(k // 512):
        a[p, :8] = np.random.permutation(np.resize(levels, 8))
        for g in range(8):
            far = levels[np.abs(levels - a[p, g]) >= 10]
            a[p, g + 8] = far[np.random.randint(len(far))]
    return np.exp2(a.ravel()).repeat(32)


def f64(x):
    return np.asarray(x).astype(np.float64)


def striped(idx):
    return np.tile(np.asarray(idx).reshape(-1, 16).T, (8, 1)).astype(np.uint16)


def unstriped(offs):
    return offs[:16].T.reshape(-1).astype(np.int64)


E2M1 = np.array([0.0, 0.5, 1.0, 1.5, 2.0, 3.0, 4.0, 6.0, -0.0, -0.5, -1.0, -1.5, -2.0, -3.0, -4.0, -6.0])


def pack_weight(w, fmt):
    k, n = w.shape
    w = f64(np.asarray(w, np.float32).astype(ml_dtypes.bfloat16)).reshape(k // 32, 32, n)
    amax = np.abs(w).max(1)
    if fmt == "e4m3":
        byte = np.frexp(amax)[1] - 1 + 127 - 7
    else:
        mant, ex = np.frexp(amax / 6.0)
        byte = np.where(mant > 0.5, ex, ex - 1) + 127
    byte = np.clip(np.where(amax > 0, byte, 1), 1, 254)
    scaled = (w * np.exp2(127.0 - byte)[:, None, :]).reshape(k, n).astype(np.float32)
    by_word = np.ascontiguousarray(scaled.reshape(k // 512, 128, 4, n).transpose(0, 1, 3, 2))
    if fmt == "e4m3":
        words = by_word.astype(ml_dtypes.float8_e4m3fn).view(np.uint8)
    else:
        c = by_word.astype(ml_dtypes.float4_e2m1fn).view(np.uint8) & 0xF
        words = (c[..., 0::2] | (c[..., 1::2] << 4)).reshape(k // 512, 128, 2 * n)
    return np.ascontiguousarray(words), np.ascontiguousarray(byte.astype(np.uint8).reshape(k // 512, 16, n))


def unpack_weight(words, scales, fmt):
    g, _, n = scales.shape
    words = np.ascontiguousarray(words).reshape(g, 128, n, -1)
    if fmt == "e4m3":
        vals = words.view(ml_dtypes.float8_e4m3fn).astype(np.float64)
    else:
        nib = np.empty((g, 128, n, 4), np.uint8)
        nib[..., 0::2] = words & 0xF
        nib[..., 1::2] = words >> 4
        vals = E2M1[nib]
    vals = vals * np.repeat(np.exp2(scales.astype(np.float64) - 127.0), 8, axis=1)[..., None]
    return vals.transpose(0, 1, 3, 2).reshape(g * 512, n)


def sigmoid(v):
    return 1.0 / (1.0 + np.exp(-v))


D, E, T, I, Q = 512, 512, 2048, 512, 128


def setup_inputs():
    n = np.random.standard_normal
    idx = np.random.permutation(T)[:I]
    fd = mx_kscale(D)
    fe = mx_kscale(E)
    keysp = pack_weight(n((D, T)) / fd[:, None], "e2m1")
    valsp = pack_weight(n((E, T)) / fe[:, None], "e2m1")
    return {
        "query": (n((D, Q)) * 0.5 / np.sqrt(D) * fd[:, None]).astype(np.float32),
        "query2": (n((D, Q)) * 0.6 / np.sqrt(D) * fd[:, None]).astype(np.float32),
        "keys_words": keysp[0],
        "keys_scales": keysp[1],
        "age": np.tile(np.random.uniform(0.0, 2.0, T), (128, 1)).astype(np.float32),
        "grace": (np.random.uniform(0.7, 1.5, (Q, 1))).astype(np.float32),
        "gout": (n((E, Q)) * 1 / np.sqrt(E) * fe[:, None]).astype(np.float32),
        "vals_words": valsp[0],
        "vals_scales": valsp[1],
        "size": (np.random.uniform(0.5, 2.0, (1, I))).astype(np.float32),
        "old": (0.5 * n((Q, T))).astype(np.float32),
        "offs": striped(idx),
    }


def reference(query, query2, keys_words, keys_scales, age, grace, gout, vals_words, vals_scales, size, old, offs):
    idx = unstriped(offs)
    keysu = unpack_weight(keys_words, keys_scales, "e2m1")
    valsu = unpack_weight(vals_words, vals_scales, "e2m1")
    queryq = mxq(f64(query), 0, "e4m3")
    keysidxg = keysu[:, idx]
    a = queryq.T @ keysidxg
    query2q = mxq(f64(query2), 0, "e4m3")
    b = query2q.T @ keysidxg
    r = np.exp(a - np.max(a, axis=1, keepdims=True))
    gt = sigmoid((b + f64(grace) - f64(age)[:1][:, idx]) * 3.0)
    p = r * gt
    z = np.sum(p, axis=1, keepdims=True)
    goutq = mxq(f64(gout), 0, "e4m3")
    valsidxg = valsu[:, idx]
    c0 = goutq.T @ valsidxg
    dz = np.sum(c0 * p * f64(size) / np.square(z) * (-1.0), axis=1, keepdims=True)
    dp = c0 / z * f64(size) + dz
    dgt = dp * r
    db = dgt * gt * (1.0 - gt) * 3.0
    gs = db * 512.0
    gf = np.zeros((Q, T))
    gf[:, idx] = gs
    y = f64(old) + gf
    return y

@@ -1,0 +1,164 @@
+from contextlib import ExitStack
+
+import concourse.mybir as mybir
+
+D, E, T, I, Q = 512, 512, 2048, 512, 128
+FLOPS = 3 * 2 * 512 * Q * I
+
+F32 = mybir.dt.float32
+BF16 = mybir.dt.bfloat16
+I32 = mybir.dt.int32
+U32 = mybir.dt.uint32
+U16 = mybir.dt.uint16
+U8 = mybir.dt.uint8
+FP8X4 = mybir.dt.float8_e4m3fn_x4
+FP4X4 = mybir.dt.float4_e2m1fn_x4
+ALU = mybir.AluOpType
+ACT = mybir.ActivationFunctionType
+AX = mybir.AxisListType
+
+P = 128
+PACK = 4
+CHUNKS = (256, 512, 512, 512, 256)
+
+
+def tile_attend_bsoftlives_b_s_kernel(
+    tc, query, query2, keys_words, keys_scales, age, grace, gout, vals_words, vals_scales, size, old, offs, out
+):
+    nc = tc.nc
+    with ExitStack() as ctx:
+        keep = ctx.enter_context(tc.tile_pool(name="keep", bufs=1))
+        psum = ctx.enter_context(tc.psum_pool(name="psum", bufs=1))
+
+        def sb(name, shape, dtype):
+            return keep.tile(shape, dtype, name=name, align_bytes=64)
+
+        offsets = sb("offsets", [P, I // 16], U16)
+        kw_pool = sb("kw_pool", [P, T], U16)
+        ks_pool = sb("ks_pool", [P, T], U8)
+        vw_pool = sb("vw_pool", [P, T], U16)
+        vs_pool = sb("vs_pool", [P, T], U8)
+        age_pool = sb("age_pool", [P, T], F32)
+        old_sb = sb("old_sb", [P, T], F32)
+        gf = sb("gf", [P, T], F32)
+        size_sb = sb("size_sb", [P, I], F32)
+        grace_sb = sb("grace_sb", [P, 1], F32)
+        raws = [sb("raw%d" % j, [P, PACK, Q], F32) for j in range(3)]
+        woven = [sb("woven%d" % j, [P, Q, PACK], BF16) for j in range(3)]
+        codes = [sb("codes%d" % j, [P, Q], U32) for j in range(3)]
+        scales = [sb("scales%d" % j, [P, Q], U8) for j in range(3)]
+        warm = sb("warm", [P, 8], F32)
+        warm_exp = sb("warm_exp", [P, 8], F32)
+        warm_sig = sb("warm_sig", [P, 8], F32)
+
+        def load_scales(pool_tile, dram):
+            for quad in range(4):
+                nc.sync.dma_start(
+                    out=pool_tile[:].bitcast(I32)[32 * quad : 32 * quad + 4, :],
+                    in_=dram[0].bitcast(I32)[4 * quad : 4 * quad + 4, :],
+                )
+
+        def load_rows(j, dram):
+            nc.sync.dma_start(out=raws[j][:], in_=dram.rearrange("(p j) w -> p j w", j=PACK))
+
+        def weave(j):
+            nc.scalar.copy(
+                out=woven[j][:].rearrange("p (c i) t -> p c t i", i=4),
+                in_=raws[j][:].rearrange("p t (c i) -> p c t i", i=4),
+            )
+
+        def quantize(j):
+            nc.vector.quantize_mx(
+                out=codes[j][:].bitcast(FP8X4), scales=scales[j][:], in_=woven[j][:].rearrange("p w t -> p (w t)")
+            )
+
+        def product(name, j, words, plane):
+            bank = psum.tile([Q, I], F32, name=name)
+            nc.tensor.matmul_mx(
+                out=bank[:],
+                lhsT=codes[j][:].bitcast(FP8X4),
+                lhsT_scale=scales[j][:],
+                rhs=words[:].bitcast(FP4X4),
+                rhs_scale=plane[:],
+                start=True,
+                stop=True,
+            )
+            return bank
+
+        def gather(name, pool_tile, dtype):
+            picked = sb(name, [P, I], dtype)
+            nc.vector.tensor_copy(picked[:], pool_tile[:].indirect(offsets[:]))
+            return picked
+
+        nc.vector.memset(ks_pool[:].bitcast(I32), 0)
+        nc.vector.memset(warm[:], 0.0)
+        nc.vector.memset(vs_pool[:].bitcast(I32), 0)
+        nc.vector.memset(gf[:], 0.0)
+        nc.scalar.activation(warm_exp[:], warm[:], ACT.Exp)
+
+        nc.sync.dma_start(offsets[:], offs)
+        load_scales(ks_pool, keys_scales)
+        nc.sync.dma_start(out=kw_pool[:].bitcast(I32), in_=keys_words[0].bitcast(I32))
+        load_rows(0, query)
+        load_rows(1, query2)
+        nc.sync.dma_start(out=vw_pool[:].bitcast(I32), in_=vals_words[0].bitcast(I32))
+        load_scales(vs_pool, vals_scales)
+        load_rows(2, gout)
+        nc.sync.dma_start(out=age_pool[:], in_=age)
+        nc.sync.dma_start(out=grace_sb[:], in_=grace)
+        nc.sync.dma_start(out=size_sb[:], in_=size[0].partition_broadcast(P))
+        nc.sync.dma_start(out=old_sb[:], in_=old)
+
+        ks = gather("ks", ks_pool, U8)
+        kw = gather("kw", kw_pool, U16)
+        weave(0)
+        weave(1)
+        quantize(0)
+        quantize(1)
+        a_ps = product("a_ps", 0, kw, ks)
+        b_ps = product("b_ps", 1, kw, ks)
+        vw = gather("vw", vw_pool, U16)
+
+        neg_max = sb("neg_max", [P, 1], F32)
+        nc.vector.tensor_reduce(neg_max[:], a_ps[:], AX.X, ALU.max, negate=True)
+        weave(2)
+        r = sb("r", [P, I], F32)
+        nc.scalar.activation(r[:], a_ps[:], ACT.Exp, bias=neg_max[:])
+        nc.scalar.activation(warm_sig[:], r[:, 0:8], ACT.Sigmoid)
+
+        vs = gather("vs", vs_pool, U8)
+        quantize(2)
+        c0_ps = product("c0_ps", 2, vw, vs)
+        age_g = gather("age_g", age_pool, F32)
+
+        life_in = sb("life_in", [P, I], F32)
+        nc.vector.scalar_tensor_tensor(life_in[:], b_ps[:], grace_sb[:], age_g[:], ALU.add, ALU.subtract)
+        gt = sb("gt", [P, I], F32)
+        nc.scalar.activation(gt[:], life_in[:], ACT.Sigmoid, scale=3.0)
+        dead = sb("dead", [P, I], F32)
+        nc.scalar.activation(dead[:], life_in[:], ACT.Sigmoid, scale=-3.0)
+
+        w = sb("w", [P, I], F32)
+        nc.vector.scalar_tensor_tensor(w[:], c0_ps[:], 1536.0, size_sb[:], ALU.mult, ALU.mult)
+        p = sb("p", [P, I], F32)
+        z = sb("z", [P, 1], F32)
+        nc.vector.scalar_tensor_tensor(p[:], r[:], 1.0, gt[:], ALU.mult, ALU.mult, accum_out=z[:])
+        rz = sb("rz", [P, 1], F32)
+        nc.vector.reciprocal(rz[:], z[:])
+        pn = sb("pn", [P, I], F32)
+        nc.scalar.activation(pn[:], p[:], ACT.Copy, scale=rz[:])
+        wp = sb("wp", [P, I], F32)
+        mean_w = sb("mean_w", [P, 1], F32)
+        nc.vector.scalar_tensor_tensor(wp[:], w[:], rz[:], p[:], ALU.mult, ALU.mult, accum_out=mean_w[:])
+        f = sb("f", [P, I], F32)
+        nc.vector.scalar_tensor_tensor(f[:], w[:], mean_w[:], dead[:], ALU.subtract, ALU.mult)
+        nc.vector.tensor_tensor(gf[:].indirect(offsets[:]), f[:], pn[:], ALU.mult)
+
+        start = 0
+        for n, width in enumerate(CHUNKS):
+            cols = slice(start, start + width)
+            res = sb("res%d" % n, [P, width], F32)
+            nc.vector.tensor_tensor(res[:], gf[:, cols], old_sb[:, cols], ALU.add)
+            queue = nc.sync if n % 2 == 0 else nc.scalar
+            queue.dma_start(out=out[:, cols], in_=res[:])
+            start = start + width

@@ -1,6 +1,7 @@
 from contextlib import ExitStack
 
 import concourse.mybir as mybir
+from concourse.masks import make_identity
 
 D, E, T, I, Q = 512, 512, 2048, 512, 128
 FLOPS = 3 * 2 * 512 * Q * I
@@ -30,26 +31,21 @@ def tile_attend_bsoftlives_b_s_kernel(
         keep = ctx.enter_context(tc.tile_pool(name="keep", bufs=1))
         psum = ctx.enter_context(tc.psum_pool(name="psum", bufs=1))
 
-        def sb(name, shape, dtype):
-            return keep.tile(shape, dtype, name=name, align_bytes=64)
+        def sb(name, shape, dtype, tag=None):
+            return keep.tile(shape, dtype, name=name, tag=tag or name, align_bytes=64)
 
         offsets = sb("offsets", [P, I // 16], U16)
         kw_pool = sb("kw_pool", [P, T], U16)
         ks_pool = sb("ks_pool", [P, T], U8)
         vw_pool = sb("vw_pool", [P, T], U16)
         vs_pool = sb("vs_pool", [P, T], U8)
-        age_pool = sb("age_pool", [P, T], F32)
-        old_sb = sb("old_sb", [P, T], F32)
-        gf = sb("gf", [P, T], F32)
-        size_sb = sb("size_sb", [P, I], F32)
-        grace_sb = sb("grace_sb", [P, 1], F32)
         raws = [sb("raw%d" % j, [P, PACK, Q], F32) for j in range(3)]
         woven = [sb("woven%d" % j, [P, Q, PACK], BF16) for j in range(3)]
         codes = [sb("codes%d" % j, [P, Q], U32) for j in range(3)]
         scales = [sb("scales%d" % j, [P, Q], U8) for j in range(3)]
         warm = sb("warm", [P, 8], F32)
         warm_exp = sb("warm_exp", [P, 8], F32)
-        warm_sig = sb("warm_sig", [P, 8], F32)
+        warm_sig = sb("warm_sig", [P, 1], F32)
 
         def load_scales(pool_tile, dram):
             for quad in range(4):
@@ -73,7 +69,7 @@ def tile_attend_bsoftlives_b_s_kernel(
             )
 
         def product(name, j, words, plane):
-            bank = psum.tile([Q, I], F32, name=name)
+            bank = psum.tile([Q, I], F32, name=name, tag=name)
             nc.tensor.matmul_mx(
                 out=bank[:],
                 lhsT=codes[j][:].bitcast(FP8X4),
@@ -85,64 +81,89 @@ def tile_attend_bsoftlives_b_s_kernel(
             )
             return bank
 
-        def gather(name, pool_tile, dtype):
-            picked = sb(name, [P, I], dtype)
+        def gather(name, pool_tile, dtype, tag=None):
+            picked = sb(name, [P, I], dtype, tag)
             nc.vector.tensor_copy(picked[:], pool_tile[:].indirect(offsets[:]))
             return picked
 
+        age_pool = sb("age_pool", [P, T], F32)
+        ident = sb("ident", [P, P], F32)
         nc.vector.memset(ks_pool[:].bitcast(I32), 0)
         nc.vector.memset(warm[:], 0.0)
+        nc.vector.memset(age_pool[:], 0.0)
         nc.vector.memset(vs_pool[:].bitcast(I32), 0)
-        nc.vector.memset(gf[:], 0.0)
         nc.scalar.activation(warm_exp[:], warm[:], ACT.Exp)
+        make_identity(nc, ident[:])
 
         nc.sync.dma_start(offsets[:], offs)
         load_scales(ks_pool, keys_scales)
         nc.sync.dma_start(out=kw_pool[:].bitcast(I32), in_=keys_words[0].bitcast(I32))
         load_rows(0, query)
         load_rows(1, query2)
+        nc.scalar.dma_start(out=age_pool[0:1, :], in_=age[0:1, :])
+        size_col = sb("size_col", [P, PACK], F32)
+        nc.sync.dma_start(out=size_col[:], in_=size.rearrange("o (p j) -> p (o j)", j=PACK))
+        load_rows(2, gout)
+        grace_sb = sb("grace_sb", [P, 1], F32)
+        nc.sync.dma_start(out=grace_sb[:], in_=grace)
         nc.sync.dma_start(out=vw_pool[:].bitcast(I32), in_=vals_words[0].bitcast(I32))
         load_scales(vs_pool, vals_scales)
-        load_rows(2, gout)
-        nc.sync.dma_start(out=age_pool[:], in_=age)
-        nc.sync.dma_start(out=grace_sb[:], in_=grace)
-        nc.sync.dma_start(out=size_sb[:], in_=size[0].partition_broadcast(P))
-        nc.sync.dma_start(out=old_sb[:], in_=old)
 
         ks = gather("ks", ks_pool, U8)
         kw = gather("kw", kw_pool, U16)
         weave(0)
-        weave(1)
         quantize(0)
-        quantize(1)
         a_ps = product("a_ps", 0, kw, ks)
+        weave(1)
+        quantize(1)
         b_ps = product("b_ps", 1, kw, ks)
-        vw = gather("vw", vw_pool, U16)
+        age_row = gather("age_row", age_pool, F32, "raw1")
 
-        neg_max = sb("neg_max", [P, 1], F32)
-        nc.vector.tensor_reduce(neg_max[:], a_ps[:], AX.X, ALU.max, negate=True)
         weave(2)
+        quantize(2)
+
+        neg_max = sb("neg_max", [P, 1], F32, "raw2")
+        nc.vector.tensor_reduce(neg_max[:], a_ps[:], AX.X, ALU.max, negate=True)
+        graced = sb("graced", [P, I], F32)
+        nc.scalar.activation(graced[:], b_ps[:], ACT.Identity, bias=grace_sb[:])
+
+        turned = psum.tile([P, I // P, P], F32, name="turned")
+        for j in range(I // P):
+            nc.tensor.transpose(turned[:, j, :], age_row[:, j * P : (j + 1) * P], ident[:])
+        age_col = sb("age_col", [P, I // P], F32)
+        nc.scalar.copy(age_col[:], turned[:, :, 0])
+        age_ps = psum.tile([P, I], F32, name="age_ps")
+        for j in range(I // P):
+            nc.tensor.transpose(age_ps[:, j * P : (j + 1) * P], age_col[:, j : j + 1].to_broadcast([P, P]), ident[:])
+
         r = sb("r", [P, I], F32)
         nc.scalar.activation(r[:], a_ps[:], ACT.Exp, bias=neg_max[:])
-        nc.scalar.activation(warm_sig[:], r[:, 0:8], ACT.Sigmoid)
+        nc.scalar.activation(warm_sig[:], turned[:, 0, 0:1], ACT.Sigmoid, bias=graced[:, 0:1], scale=r[:, 0:1])
 
-        vs = gather("vs", vs_pool, U8)
-        quantize(2)
-        c0_ps = product("c0_ps", 2, vw, vs)
-        age_g = gather("age_g", age_pool, F32)
-
-        life_in = sb("life_in", [P, I], F32)
-        nc.vector.scalar_tensor_tensor(life_in[:], b_ps[:], grace_sb[:], age_g[:], ALU.add, ALU.subtract)
+        vw = gather("vw", vw_pool, U16, "woven2")
+        old_sb = sb("old_sb", [P, T], F32, "vw_pool")
+        nc.sync.dma_start(out=old_sb[:], in_=old)
+        life = sb("life", [P, I], F32)
+        nc.vector.tensor_tensor(life[:], graced[:], age_ps[:], ALU.subtract)
         gt = sb("gt", [P, I], F32)
-        nc.scalar.activation(gt[:], life_in[:], ACT.Sigmoid, scale=3.0)
+        nc.scalar.activation(gt[:], life[:], ACT.Sigmoid, scale=3.0)
+        size_ps = psum.tile([P, PACK, P], F32, name="size_ps", tag="a_ps")
+        for j in range(PACK):
+            nc.tensor.transpose(size_ps[:, j, :], size_col[:, j : j + 1].to_broadcast([P, P]), ident[:])
+        size_sb = sb("size_sb", [P, I], F32, "graced")
+        nc.scalar.copy(size_sb[:].rearrange("q (p j) -> q p j", j=PACK), size_ps[:].rearrange("q j p -> q p j"))
         dead = sb("dead", [P, I], F32)
-        nc.scalar.activation(dead[:], life_in[:], ACT.Sigmoid, scale=-3.0)
+        nc.scalar.activation(dead[:], life[:], ACT.Sigmoid, scale=-3.0)
+        vs = gather("vs", vs_pool, U8, "age_col")
+        c0_ps = product("c0_ps", 2, vw, vs)
+        gf = sb("gf", [P, T], F32, "vs_pool")
+        nc.gpsimd.memset(gf[:], 0.0)
 
-        w = sb("w", [P, I], F32)
-        nc.vector.scalar_tensor_tensor(w[:], c0_ps[:], 1536.0, size_sb[:], ALU.mult, ALU.mult)
         p = sb("p", [P, I], F32)
         z = sb("z", [P, 1], F32)
         nc.vector.scalar_tensor_tensor(p[:], r[:], 1.0, gt[:], ALU.mult, ALU.mult, accum_out=z[:])
+        w = sb("w", [P, I], F32)
+        nc.vector.scalar_tensor_tensor(w[:], c0_ps[:], 1536.0, size_sb[:], ALU.mult, ALU.mult)
         rz = sb("rz", [P, 1], F32)
         nc.vector.reciprocal(rz[:], z[:])
         pn = sb("pn", [P, I], F32)

@@ -97,8 +97,8 @@ def tile_attend_bsoftlives_b_s_kernel(
 
         nc.sync.dma_start(offsets[:], offs)
         load_scales(ks_pool, keys_scales)
-        nc.sync.dma_start(out=kw_pool[:].bitcast(I32), in_=keys_words[0].bitcast(I32))
         load_rows(0, query)
+        nc.sync.dma_start(out=kw_pool[:].bitcast(I32), in_=keys_words[0].bitcast(I32))
         load_rows(1, query2)
         nc.scalar.dma_start(out=age_pool[0:1, :], in_=age[0:1, :])
         size_col = sb("size_col", [P, PACK], F32)

from contextlib import ExitStack

import concourse.mybir as mybir
from concourse.masks import make_identity

D, E, T, I, Q = 512, 512, 2048, 512, 128
FLOPS = 3 * 2 * 512 * Q * I

F32 = mybir.dt.float32
BF16 = mybir.dt.bfloat16
I32 = mybir.dt.int32
U32 = mybir.dt.uint32
U16 = mybir.dt.uint16
U8 = mybir.dt.uint8
FP8X4 = mybir.dt.float8_e4m3fn_x4
FP4X4 = mybir.dt.float4_e2m1fn_x4
ALU = mybir.AluOpType
ACT = mybir.ActivationFunctionType
AX = mybir.AxisListType

P = 128
PACK = 4
CHUNKS = (256, 512, 512, 512, 256)


def tile_attend_bsoftlives_b_s_kernel(
    tc, query, query2, keys_words, keys_scales, age, grace, gout, vals_words, vals_scales, size, old, offs, out
):
    nc = tc.nc
    with ExitStack() as ctx:
        keep = ctx.enter_context(tc.tile_pool(name="keep", bufs=1))
        psum = ctx.enter_context(tc.psum_pool(name="psum", bufs=1))

        def sb(name, shape, dtype, tag=None):
            return keep.tile(shape, dtype, name=name, tag=tag or name, align_bytes=64)

        offsets = sb("offsets", [P, I // 16], U16)
        kw_pool = sb("kw_pool", [P, T], U16)
        ks_pool = sb("ks_pool", [P, T], U8)
        vw_pool = sb("vw_pool", [P, T], U16)
        vs_pool = sb("vs_pool", [P, T], U8)
        raws = [sb("raw%d" % j, [P, PACK, Q], F32) for j in range(3)]
        woven = [sb("woven%d" % j, [P, Q, PACK], BF16) for j in range(3)]
        codes = [sb("codes%d" % j, [P, Q], U32) for j in range(3)]
        scales = [sb("scales%d" % j, [P, Q], U8) for j in range(3)]
        warm = sb("warm", [P, 8], F32)
        warm_exp = sb("warm_exp", [P, 8], F32)
        warm_sig = sb("warm_sig", [P, 1], F32)

        def load_scales(pool_tile, dram):
            for quad in range(4):
                nc.sync.dma_start(
                    out=pool_tile[:].bitcast(I32)[32 * quad : 32 * quad + 4, :],
                    in_=dram[0].bitcast(I32)[4 * quad : 4 * quad + 4, :],
                )

        def load_rows(j, dram):
            nc.sync.dma_start(out=raws[j][:], in_=dram.rearrange("(p j) w -> p j w", j=PACK))

        def weave(j):
            nc.scalar.copy(
                out=woven[j][:].rearrange("p (c i) t -> p c t i", i=4),
                in_=raws[j][:].rearrange("p t (c i) -> p c t i", i=4),
            )

        def quantize(j):
            nc.vector.quantize_mx(
                out=codes[j][:].bitcast(FP8X4), scales=scales[j][:], in_=woven[j][:].rearrange("p w t -> p (w t)")
            )

        def product(name, j, words, plane):
            bank = psum.tile([Q, I], F32, name=name, tag=name)
            nc.tensor.matmul_mx(
                out=bank[:],
                lhsT=codes[j][:].bitcast(FP8X4),
                lhsT_scale=scales[j][:],
                rhs=words[:].bitcast(FP4X4),
                rhs_scale=plane[:],
                start=True,
                stop=True,
            )
            return bank

        def gather(name, pool_tile, dtype, tag=None):
            picked = sb(name, [P, I], dtype, tag)
            nc.vector.tensor_copy(picked[:], pool_tile[:].indirect(offsets[:]))
            return picked

        age_pool = sb("age_pool", [P, T], F32)
        ident = sb("ident", [P, P], F32)
        nc.vector.memset(ks_pool[:].bitcast(I32), 0)
        nc.vector.memset(warm[:], 0.0)
        nc.vector.memset(age_pool[:], 0.0)
        nc.vector.memset(vs_pool[:].bitcast(I32), 0)
        nc.scalar.activation(warm_exp[:], warm[:], ACT.Exp)
        make_identity(nc, ident[:])

        nc.sync.dma_start(offsets[:], offs)
        load_scales(ks_pool, keys_scales)
        load_rows(0, query)
        nc.sync.dma_start(out=kw_pool[:].bitcast(I32), in_=keys_words[0].bitcast(I32))
        load_rows(1, query2)
        nc.scalar.dma_start(out=age_pool[0:1, :], in_=age[0:1, :])
        size_col = sb("size_col", [P, PACK], F32)
        nc.sync.dma_start(out=size_col[:], in_=size.rearrange("o (p j) -> p (o j)", j=PACK))
        load_rows(2, gout)
        grace_sb = sb("grace_sb", [P, 1], F32)
        nc.sync.dma_start(out=grace_sb[:], in_=grace)
        nc.sync.dma_start(out=vw_pool[:].bitcast(I32), in_=vals_words[0].bitcast(I32))
        load_scales(vs_pool, vals_scales)

        ks = gather("ks", ks_pool, U8)
        kw = gather("kw", kw_pool, U16)
        weave(0)
        quantize(0)
        a_ps = product("a_ps", 0, kw, ks)
        weave(1)
        quantize(1)
        b_ps = product("b_ps", 1, kw, ks)
        age_row = gather("age_row", age_pool, F32, "raw1")

        weave(2)
        quantize(2)

        neg_max = sb("neg_max", [P, 1], F32, "raw2")
        nc.vector.tensor_reduce(neg_max[:], a_ps[:], AX.X, ALU.max, negate=True)
        graced = sb("graced", [P, I], F32)
        nc.scalar.activation(graced[:], b_ps[:], ACT.Identity, bias=grace_sb[:])

        turned = psum.tile([P, I // P, P], F32, name="turned")
        for j in range(I // P):
            nc.tensor.transpose(turned[:, j, :], age_row[:, j * P : (j + 1) * P], ident[:])
        age_col = sb("age_col", [P, I // P], F32)
        nc.scalar.copy(age_col[:], turned[:, :, 0])
        age_ps = psum.tile([P, I], F32, name="age_ps")
        for j in range(I // P):
            nc.tensor.transpose(age_ps[:, j * P : (j + 1) * P], age_col[:, j : j + 1].to_broadcast([P, P]), ident[:])

        r = sb("r", [P, I], F32)
        nc.scalar.activation(r[:], a_ps[:], ACT.Exp, bias=neg_max[:])
        nc.scalar.activation(warm_sig[:], turned[:, 0, 0:1], ACT.Sigmoid, bias=graced[:, 0:1], scale=r[:, 0:1])

        vw = gather("vw", vw_pool, U16, "woven2")
        old_sb = sb("old_sb", [P, T], F32, "vw_pool")
        nc.sync.dma_start(out=old_sb[:], in_=old)
        life = sb("life", [P, I], F32)
        nc.vector.tensor_tensor(life[:], graced[:], age_ps[:], ALU.subtract)
        gt = sb("gt", [P, I], F32)
        nc.scalar.activation(gt[:], life[:], ACT.Sigmoid, scale=3.0)
        size_ps = psum.tile([P, PACK, P], F32, name="size_ps", tag="a_ps")
        for j in range(PACK):
            nc.tensor.transpose(size_ps[:, j, :], size_col[:, j : j + 1].to_broadcast([P, P]), ident[:])
        size_sb = sb("size_sb", [P, I], F32, "graced")
        nc.scalar.copy(size_sb[:].rearrange("q (p j) -> q p j", j=PACK), size_ps[:].rearrange("q j p -> q p j"))
        dead = sb("dead", [P, I], F32)
        nc.scalar.activation(dead[:], life[:], ACT.Sigmoid, scale=-3.0)
        vs = gather("vs", vs_pool, U8, "age_col")
        c0_ps = product("c0_ps", 2, vw, vs)
        gf = sb("gf", [P, T], F32, "vs_pool")
        nc.gpsimd.memset(gf[:], 0.0)

        p = sb("p", [P, I], F32)
        z = sb("z", [P, 1], F32)
        nc.vector.scalar_tensor_tensor(p[:], r[:], 1.0, gt[:], ALU.mult, ALU.mult, accum_out=z[:])
        w = sb("w", [P, I], F32)
        nc.vector.scalar_tensor_tensor(w[:], c0_ps[:], 1536.0, size_sb[:], ALU.mult, ALU.mult)
        rz = sb("rz", [P, 1], F32)
        nc.vector.reciprocal(rz[:], z[:])
        pn = sb("pn", [P, I], F32)
        nc.scalar.activation(pn[:], p[:], ACT.Copy, scale=rz[:])
        wp = sb("wp", [P, I], F32)
        mean_w = sb("mean_w", [P, 1], F32)
        nc.vector.scalar_tensor_tensor(wp[:], w[:], rz[:], p[:], ALU.mult, ALU.mult, accum_out=mean_w[:])
        f = sb("f", [P, I], F32)
        nc.vector.scalar_tensor_tensor(f[:], w[:], mean_w[:], dead[:], ALU.subtract, ALU.mult)
        nc.vector.tensor_tensor(gf[:].indirect(offsets[:]), f[:], pn[:], ALU.mult)

        start = 0
        for n, width in enumerate(CHUNKS):
            cols = slice(start, start + width)
            res = sb("res%d" % n, [P, width], F32)
            nc.vector.tensor_tensor(res[:], gf[:, cols], old_sb[:, cols], ALU.add)
            queue = nc.sync if n % 2 == 0 else nc.scalar
            queue.dma_start(out=out[:, cols], in_=res[:])
            start = start + width
